import numpy as np
import ml_dtypes


def mxq(x, axis, fmt="e4m3"):
    dtype, down = {"e4m3": (ml_dtypes.float8_e4m3fn, 7), "e5m2": (ml_dtypes.float8_e5m2, 14)}[fmt]
    v = np.moveaxis(np.asarray(x, np.float32).astype(ml_dtypes.bfloat16).astype(np.float64), axis, -1)
    blocks = v.reshape(v.shape[:-1] + (-1, 32))
    amax = np.abs(blocks).max(-1, keepdims=True)
    byte = np.maximum(np.where(amax > 0, np.frexp(amax)[1] - 1 + 127, 0) - down, 1)
    scale = np.exp2(byte - 127.0)
    codes = (blocks / scale).astype(np.float32).astype(dtype).astype(np.float64)
    return np.moveaxis((codes * scale).reshape(v.shape), -1, axis)


WIDE = False


def mx_kscale(k):
    if not WIDE:
        return np.ones(k)
    levels = np.array([10, -10, 5, -5, 0])
    if k % 512:
        return np.exp2(np.random.permutation(np.resize(levels, k // 32))).repeat(32)
    a = np.empty((k // 512, 16))
    for p in range(k // 512):
        a[p, :8] = np.random.permutation(np.resize(levels, 8))
        for g in range(8):
            far = levels[np.abs(levels - a[p, g]) >= 10]
            a[p, g + 8] = far[np.random.randint(len(far))]
    return np.exp2(a.ravel()).repeat(32)


def f64(x):
    return np.asarray(x).astype(np.float64)


def striped(idx):
    return np.tile(idx.reshape(-1, 16).T, (8, 1)).astype(np.uint16)


def unstriped(offs):
    return offs[:16].T.reshape(-1).astype(np.int64)


def pack_weight(w):
    k, n = w.shape
    w = f64(np.asarray(w, np.float32).astype(ml_dtypes.bfloat16)).reshape(k // 32, 32, n)
    amax = np.abs(w).max(1)
    byte = np.clip(np.where(amax > 0, np.frexp(amax)[1] - 1 + 127 - 7, 1), 1, 254)
    scaled = (w * np.exp2(127.0 - byte)[:, None, :]).reshape(k, n).astype(np.float32)
    words = np.ascontiguousarray(scaled.reshape(k // 512, 128, 4, n).transpose(0, 1, 3, 2)).astype(ml_dtypes.float8_e4m3fn).view(np.uint8)
    return words, np.ascontiguousarray(byte.astype(np.uint8).reshape(k // 512, 16, n))


def unpack_weight(words, scales):
    g, p, n, _ = words.shape
    vals = np.ascontiguousarray(words).view(ml_dtypes.float8_e4m3fn).astype(np.float64) * np.repeat(np.exp2(scales.astype(np.float64) - 127.0), 8, axis=1)[..., None]
    return vals.transpose(0, 1, 3, 2).reshape(g * 512, n)


def sigmoid(v):
    return 1.0 / (1.0 + np.exp(-np.maximum(v, -700.0)))


K, T, S, N = 512, 2048, 512, 256
P = 2 ** 7


def setup_inputs():
    n = np.random.standard_normal
    s = mx_kscale(K)[:, None]
    packed_xT = pack_weight(n((K, T)) * s)
    return {
        "x_words": packed_xT[0],
        "x_scales": packed_xT[1],
        "w1": (n((K, N)) / np.sqrt(K) / s).astype(np.float32),
        "w2": (n((K, N)) / np.sqrt(K) / s).astype(np.float32),
        "offset": (np.tile(0.5 * n(S), (P, 1))).astype(np.float32),
        "lab": (np.tile((np.random.uniform(size=S) < 0.5) * 1.0, (P, 1))).astype(np.float32),
        "offs": striped(np.random.permutation(T)[:S]),
    }


def reference(x_words, x_scales, w1, w2, offset, lab, offs):
    xq = unpack_weight(x_words, x_scales)[:, unstriped(offs)]
    ym = mxq(f64(w1), 0, "e4m3").T @ xq
    ys = mxq(f64(w2), 0, "e4m3").T @ xq
    sd = 0.8 * (np.log(np.exp(ys) + 1.0)) + 0.3
    s0 = sigmoid(ym + f64(offset)[:1] + -2.3344 * sd)
    s1 = sigmoid(ym + f64(offset)[:1] + -0.7420 * sd)
    s2 = sigmoid(ym + f64(offset)[:1] + 0.7420 * sd)
    s3 = sigmoid(ym + f64(offset)[:1] + 2.3344 * sd)
    pm = 0.0459 * s0 + 0.4541 * s1 + 0.4541 * s2 + 0.0459 * s3
    return -1.0 * (f64(lab)[:1] * np.log(pm + 0.001) + (-1.0 * f64(lab)[:1] + 1.0) * np.log(-1.0 * pm + 1.001))

@@ -1,0 +1,184 @@
+from contextlib import ExitStack
+
+import concourse.mybir as mybir
+from concourse.masks import make_identity
+
+K, T, S, N = 512, 2048, 512, 256
+FLOPS = 2 * 2 * K * N * S
+BYTES = K * T + 16 * T + 2 * K * N * 4 + 2 * S * 4 + 128 * 32 * 2 + N * S * 4
+
+F32 = mybir.dt.float32
+BF16 = mybir.dt.bfloat16
+I32 = mybir.dt.int32
+U32 = mybir.dt.uint32
+U16 = mybir.dt.uint16
+U8 = mybir.dt.uint8
+FP8X4 = mybir.dt.float8_e4m3fn_x4
+ALU = mybir.AluOpType
+ACT = mybir.ActivationFunctionType
+
+P = 128
+TILES = S // P
+HALVES = N // P
+PAIRS = 2
+NODES = (-2.3344, 2.3344, -0.7420, 0.7420)
+W_OUTER, W_INNER = 0.0459, 0.4541
+TINY = 2.0 ** -60
+
+
+def tile_picked_yghqlr_nll_p_kernel(tc, x_words, x_scales, w1, w2, offset, lab, offs, out):
+    nc = tc.nc
+    with ExitStack() as ctx:
+        sb = ctx.enter_context(tc.tile_pool(name="sb", bufs=1))
+        ps = ctx.enter_context(tc.psum_pool(name="ps", bufs=1))
+
+        offsets = sb.tile([P, S // 16], U16, name="offsets")
+        nc.sync.dma_start(offsets[:], offs)
+
+        scale_table = sb.tile([P, T], U8, name="scale_table", align_bytes=64)
+        nc.vector.memset(scale_table[:].bitcast(I32), 0)
+
+        w2_raw = sb.tile([P, 4, N], F32, name="w2_raw")
+        nc.sync.dma_start(w2_raw[:], w2.rearrange("(p j) n -> p j n", j=4))
+        for r in range(4):
+            nc.sync.dma_start(scale_table[r:P:32, :].bitcast(I32), x_scales[0, r:16:4, :].bitcast(I32))
+        word_table = sb.tile([P, T], I32, name="word_table", align_bytes=64)
+        nc.sync.dma_start(word_table[:], x_words[0].rearrange("p c r -> p (c r)").bitcast(I32))
+        w1_raw = sb.tile([P, 4, N], F32, name="w1_raw")
+        nc.sync.dma_start(w1_raw[:], w1.rearrange("(p j) n -> p j n", j=4))
+
+        ident = sb.tile([P, P], F32, name="ident")
+        make_identity(nc, ident[:])
+        rows = sb.tile([P, P], F32, name="rows")
+        nc.gpsimd.memset(rows[:], 0.0)
+        nc.sync.dma_start(rows[0:TILES, :], offset[0].rearrange("(t p) -> t p", p=P))
+        nc.sync.dma_start(rows[TILES : 2 * TILES, :], lab[0].rearrange("(t p) -> t p", p=P))
+
+        def interleave(raw, name):
+            grouped = sb.tile([P, N, 4], BF16, name=name + "_grouped", align_bytes=64)
+            nc.vector.tensor_copy(
+                out=grouped[:].rearrange("p (c i) j -> p c j i", i=4),
+                in_=raw[:].rearrange("p j (c i) -> p c j i", i=4),
+            )
+            return grouped
+
+        def quantize(grouped, name):
+            codes = sb.tile([P, N], U32, name=name + "_codes", align_bytes=64)
+            scales = sb.tile([P, N], U8, name=name + "_scales", align_bytes=64)
+            nc.vector.quantize_mx(out=codes[:].bitcast(FP8X4), scales=scales[:], in_=grouped[:].rearrange("p n j -> p (n j)"))
+            return codes, scales
+
+        w2_grouped = interleave(w2_raw, "w2")
+        x_scale = sb.tile([P, S], U8, name="x_scale", align_bytes=64)
+        nc.vector.tensor_copy(x_scale[:], scale_table[:].indirect(offsets[:]))
+        w2_codes, w2_scales = quantize(w2_grouped, "w2")
+
+        def product(bank, x_codes, a, codes, scales):
+            for i in range(2):
+                t = 2 * a + i
+                nc.tensor.matmul_mx(
+                    out=bank[:, i, :],
+                    lhsT=x_codes[:, i * P : (i + 1) * P].bitcast(FP8X4),
+                    lhsT_scale=x_scale[:, t * P : (t + 1) * P],
+                    rhs=codes[:].bitcast(FP8X4),
+                    rhs_scale=scales[:],
+                    start=True,
+                    stop=True,
+                )
+
+        def work(name):
+            return sb.tile([P, HALVES, TILES, P], F32, name=name)
+
+        sig_neg = work("sig_neg")
+        x_pair, ys = [], []
+        for a in range(PAIRS):
+            x_codes = sb.tile([P, 2 * P], U32, name="x_codes%d" % a, align_bytes=64)
+            nc.vector.tensor_copy(x_codes[:], word_table[:].bitcast(U32).indirect(offsets[:, 16 * a : 16 * (a + 1)]))
+            bank = ps.tile([P, 2, N], F32, name="ys%d" % a)
+            product(bank, x_codes, a, w2_codes, w2_scales)
+            nc.scalar.activation(
+                out=sig_neg[:, :, 2 * a : 2 * a + 2, :].rearrange("p h t m -> p t h m"),
+                in_=bank[:].rearrange("p t (h m) -> p t h m", h=HALVES),
+                func=ACT.Sigmoid,
+                scale=-1.0,
+            )
+            x_pair.append(x_codes)
+            ys.append(bank)
+
+        cols_bank = ps.tile([P, P], F32, name="cols_bank")
+        nc.tensor.transpose(cols_bank[:], rows[:], ident[:])
+        off_col = sb.tile([P, TILES], F32, name="off_col")
+        sign_col = sb.tile([P, TILES], F32, name="sign_col")
+
+        w1_grouped = interleave(w1_raw, "w1")
+        nc.vector.tensor_copy(off_col[:], cols_bank[:, 0:TILES])
+        nc.vector.tensor_scalar(sign_col[:], cols_bank[:, TILES : 2 * TILES], 2.0, -1.0, ALU.mult, ALU.add)
+        w1_codes, w1_scales = quantize(w1_grouped, "w1")
+
+        mean = work("mean")
+        for a in range(PAIRS):
+            bank = ps.tile([P, 2, N], F32, name="ym%d" % a)
+            product(bank, x_pair[a], a, w1_codes, w1_scales)
+            for i in range(2):
+                t = 2 * a + i
+                nc.vector.tensor_scalar(
+                    mean[:, :, t, :],
+                    bank[:, i, :].rearrange("p (h m) -> p h m", h=HALVES),
+                    off_col[:, t : t + 1],
+                    sign_col[:, t : t + 1],
+                    ALU.add,
+                    ALU.mult,
+                )
+
+        log_sig = work("log_sig")
+        soft = work("soft")
+        for h in range(HALVES):
+            nc.scalar.activation(out=log_sig[:, h], in_=sig_neg[:, h], func=ACT.Ln, bias=TINY)
+            for a in range(PAIRS):
+                nc.vector.scalar_tensor_tensor(
+                    out=soft[:, h, 2 * a : 2 * a + 2, :],
+                    in0=log_sig[:, h, 2 * a : 2 * a + 2, :],
+                    scalar=-1.0,
+                    in1=ys[a][:, :, h * P : (h + 1) * P],
+                    op0=ALU.mult,
+                    op1=ALU.max,
+                )
+
+        args = [work("arg%d" % i) for i in range(4)]
+        sigs = [work("sig%d" % i) for i in range(4)]
+        for h in range(HALVES):
+            for i, c in enumerate(NODES):
+                nc.vector.scalar_tensor_tensor(
+                    out=args[i][:, h], in0=soft[:, h], scalar=0.8 * c, in1=mean[:, h], op0=ALU.mult, op1=ALU.add
+                )
+                nc.scalar.activation(out=sigs[i][:, h], in_=args[i][:, h], func=ACT.Sigmoid, bias=0.3 * c)
+
+        outer = work("outer")
+        three = work("three")
+        totals = []
+        for h in range(HALVES):
+            nc.vector.tensor_tensor(outer[:, h], sigs[0][:, h], sigs[1][:, h], ALU.add)
+            nc.vector.scalar_tensor_tensor(
+                out=three[:, h], in0=outer[:, h], scalar=W_OUTER / W_INNER, in1=sigs[2][:, h], op0=ALU.mult, op1=ALU.add
+            )
+            total = ps.tile([P, S], F32, name="total%d" % h)
+            for j, part in enumerate((sigs[3], three)):
+                for t in range(TILES):
+                    nc.tensor.matmul(
+                        total[:, t * P : (t + 1) * P],
+                        lhsT=part[:, h, t, :],
+                        rhs=ident[:],
+                        is_transpose=True,
+                        start=(j == 0 and t == 0),
+                        stop=(j == 1 and t == TILES - 1),
+                    )
+            totals.append(total)
+
+        for h in range(HALVES):
+            for a in range(PAIRS):
+                cols = slice(2 * P * a, 2 * P * (a + 1))
+                logp = sb.tile([P, 2 * P], F32, name="logp%d%d" % (h, a))
+                nc.scalar.activation(out=logp[:], in_=totals[h][:, cols], func=ACT.Ln, scale=W_INNER, bias=0.001)
+                nll = sb.tile([P, 2 * P], F32, name="nll%d%d" % (h, a))
+                nc.vector.tensor_scalar(nll[:], logp[:], -1.0, None, ALU.mult)
+                nc.sync.dma_start(out[h * P : (h + 1) * P, cols], nll[:])

@@ -32,16 +32,15 @@ def tile_picked_yghqlr_nll_p_kernel(tc, x_words, x_scales, w1, w2, offset, lab, 
         sb = ctx.enter_context(tc.tile_pool(name="sb", bufs=1))
         ps = ctx.enter_context(tc.psum_pool(name="ps", bufs=1))
 
-        offsets = sb.tile([P, S // 16], U16, name="offsets")
-        nc.sync.dma_start(offsets[:], offs)
-
         scale_table = sb.tile([P, T], U8, name="scale_table", align_bytes=64)
-        nc.vector.memset(scale_table[:].bitcast(I32), 0)
+        nc.gpsimd.memset(scale_table[:].bitcast(I32), 0)
 
         w2_raw = sb.tile([P, 4, N], F32, name="w2_raw")
         nc.sync.dma_start(w2_raw[:], w2.rearrange("(p j) n -> p j n", j=4))
         for r in range(4):
             nc.sync.dma_start(scale_table[r:P:32, :].bitcast(I32), x_scales[0, r:16:4, :].bitcast(I32))
+        offsets = sb.tile([P, S // 16], U16, name="offsets")
+        nc.sync.dma_start(offsets[:], offs)
         word_table = sb.tile([P, T], I32, name="word_table", align_bytes=64)
         nc.sync.dma_start(word_table[:], x_words[0].rearrange("p c r -> p (c r)").bitcast(I32))
         w1_raw = sb.tile([P, 4, N], F32, name="w1_raw")
@@ -73,37 +72,30 @@ def tile_picked_yghqlr_nll_p_kernel(tc, x_words, x_scales, w1, w2, offset, lab, 
         nc.vector.tensor_copy(x_scale[:], scale_table[:].indirect(offsets[:]))
         w2_codes, w2_scales = quantize(w2_grouped, "w2")
 
-        def product(bank, x_codes, a, codes, scales):
-            for i in range(2):
-                t = 2 * a + i
-                nc.tensor.matmul_mx(
-                    out=bank[:, i, :],
-                    lhsT=x_codes[:, i * P : (i + 1) * P].bitcast(FP8X4),
-                    lhsT_scale=x_scale[:, t * P : (t + 1) * P],
-                    rhs=codes[:].bitcast(FP8X4),
-                    rhs_scale=scales[:],
-                    start=True,
-                    stop=True,
-                )
+        def product(dst, x_codes, t, codes, scales):
+            nc.tensor.matmul_mx(
+                out=dst,
+                lhsT=x_codes[:].bitcast(FP8X4),
+                lhsT_scale=x_scale[:, t * P : (t + 1) * P],
+                rhs=codes[:].bitcast(FP8X4),
+                rhs_scale=scales[:],
+                start=True,
+                stop=True,
+            )
 
         def work(name):
-            return sb.tile([P, HALVES, TILES, P], F32, name=name)
+            return sb.tile([P, TILES, N], F32, name=name)
 
         sig_neg = work("sig_neg")
-        x_pair, ys = [], []
-        for a in range(PAIRS):
-            x_codes = sb.tile([P, 2 * P], U32, name="x_codes%d" % a, align_bytes=64)
-            nc.vector.tensor_copy(x_codes[:], word_table[:].bitcast(U32).indirect(offsets[:, 16 * a : 16 * (a + 1)]))
-            bank = ps.tile([P, 2, N], F32, name="ys%d" % a)
-            product(bank, x_codes, a, w2_codes, w2_scales)
-            nc.scalar.activation(
-                out=sig_neg[:, :, 2 * a : 2 * a + 2, :].rearrange("p h t m -> p t h m"),
-                in_=bank[:].rearrange("p t (h m) -> p t h m", h=HALVES),
-                func=ACT.Sigmoid,
-                scale=-1.0,
-            )
-            x_pair.append(x_codes)
-            ys.append(bank)
+        x_tiles, banks = [], []
+        for t in range(TILES):
+            x_codes = sb.tile([P, P], U32, name="x_codes%d" % t, align_bytes=64)
+            nc.vector.tensor_copy(x_codes[:], word_table[:].bitcast(U32).indirect(offsets[:, 8 * t : 8 * (t + 1)]))
+            bank = ps.tile([P, 2, N], F32, name="y%d" % t)
+            product(bank[:, 0, :], x_codes, t, w2_codes, w2_scales)
+            nc.scalar.activation(out=sig_neg[:, t, :], in_=bank[:, 0, :], func=ACT.Sigmoid, scale=-1.0)
+            x_tiles.append(x_codes)
+            banks.append(bank)
 
         cols_bank = ps.tile([P, P], F32, name="cols_bank")
         nc.tensor.transpose(cols_bank[:], rows[:], ident[:])
@@ -116,69 +108,69 @@ def tile_picked_yghqlr_nll_p_kernel(tc, x_words, x_scales, w1, w2, offset, lab, 
         w1_codes, w1_scales = quantize(w1_grouped, "w1")
 
         mean = work("mean")
-        for a in range(PAIRS):
-            bank = ps.tile([P, 2, N], F32, name="ym%d" % a)
-            product(bank, x_pair[a], a, w1_codes, w1_scales)
-            for i in range(2):
-                t = 2 * a + i
-                nc.vector.tensor_scalar(
-                    mean[:, :, t, :],
-                    bank[:, i, :].rearrange("p (h m) -> p h m", h=HALVES),
-                    off_col[:, t : t + 1],
-                    sign_col[:, t : t + 1],
-                    ALU.add,
-                    ALU.mult,
-                )
+        for t in range(TILES):
+            product(banks[t][:, 1, :], x_tiles[t], t, w1_codes, w1_scales)
+            nc.vector.tensor_scalar(
+                mean[:, t, :], banks[t][:, 1, :], off_col[:, t : t + 1], sign_col[:, t : t + 1], ALU.add, ALU.mult
+            )
 
         log_sig = work("log_sig")
         soft = work("soft")
-        for h in range(HALVES):
-            nc.scalar.activation(out=log_sig[:, h], in_=sig_neg[:, h], func=ACT.Ln, bias=TINY)
-            for a in range(PAIRS):
-                nc.vector.scalar_tensor_tensor(
-                    out=soft[:, h, 2 * a : 2 * a + 2, :],
-                    in0=log_sig[:, h, 2 * a : 2 * a + 2, :],
-                    scalar=-1.0,
-                    in1=ys[a][:, :, h * P : (h + 1) * P],
-                    op0=ALU.mult,
-                    op1=ALU.max,
-                )
+        for t in range(TILES):
+            nc.scalar.activation(out=log_sig[:, t, :], in_=sig_neg[:, t, :], func=ACT.Ln, bias=TINY)
+            nc.vector.scalar_tensor_tensor(
+                out=soft[:, t, :], in0=log_sig[:, t, :], scalar=-1.0, in1=banks[t][:, 0, :], op0=ALU.mult, op1=ALU.max
+            )
 
+        pairs = [slice(2 * a, 2 * a + 2) for a in range(PAIRS)]
         args = [work("arg%d" % i) for i in range(4)]
         sigs = [work("sig%d" % i) for i in range(4)]
-        for h in range(HALVES):
+        for a in range(PAIRS):
             for i, c in enumerate(NODES):
                 nc.vector.scalar_tensor_tensor(
-                    out=args[i][:, h], in0=soft[:, h], scalar=0.8 * c, in1=mean[:, h], op0=ALU.mult, op1=ALU.add
+                    out=args[i][:, pairs[a]],
+                    in0=soft[:, pairs[a]],
+                    scalar=0.8 * c,
+                    in1=mean[:, pairs[a]],
+                    op0=ALU.mult,
+                    op1=ALU.add,
                 )
-                nc.scalar.activation(out=sigs[i][:, h], in_=args[i][:, h], func=ACT.Sigmoid, bias=0.3 * c)
+                nc.scalar.activation(out=sigs[i][:, pairs[a]], in_=args[i][:, pairs[a]], func=ACT.Sigmoid, bias=0.3 * c)
+
+        totals = [ps.tile([P, HALVES, 2 * P], F32, name="total%d" % a) for a in range(PAIRS)]
+
+        def add_turned(part, a, first, last):
+            for h in range(HALVES):
+                for i in range(2):
+                    nc.tensor.matmul(
+                        totals[a][:, h, i * P : (i + 1) * P],
+                        lhsT=part[:, 2 * a + i, h * P : (h + 1) * P],
+                        rhs=ident[:],
+                        is_transpose=True,
+                        start=(first and h == 0 and i == 0),
+                        stop=(last and h == HALVES - 1 and i == 1),
+                    )
 
         outer = work("outer")
         three = work("three")
-        totals = []
-        for h in range(HALVES):
-            nc.vector.tensor_tensor(outer[:, h], sigs[0][:, h], sigs[1][:, h], ALU.add)
+        for a in range(PAIRS):
+            nc.vector.tensor_tensor(outer[:, pairs[a]], sigs[0][:, pairs[a]], sigs[1][:, pairs[a]], ALU.add)
+            add_turned(sigs[3], a, True, False)
+        for a in range(PAIRS):
             nc.vector.scalar_tensor_tensor(
-                out=three[:, h], in0=outer[:, h], scalar=W_OUTER / W_INNER, in1=sigs[2][:, h], op0=ALU.mult, op1=ALU.add
+                out=three[:, pairs[a]],
+                in0=outer[:, pairs[a]],
+                scalar=W_OUTER / W_INNER,
+                in1=sigs[2][:, pairs[a]],
+                op0=ALU.mult,
+                op1=ALU.add,
             )
-            total = ps.tile([P, S], F32, name="total%d" % h)
-            for j, part in enumerate((sigs[3], three)):
-                for t in range(TILES):
-                    nc.tensor.matmul(
-                        total[:, t * P : (t + 1) * P],
-                        lhsT=part[:, h, t, :],
-                        rhs=ident[:],
-                        is_transpose=True,
-                        start=(j == 0 and t == 0),
-                        stop=(j == 1 and t == TILES - 1),
-                    )
-            totals.append(total)
+            add_turned(three, a, False, True)
 
-        for h in range(HALVES):
-            for a in range(PAIRS):
-                cols = slice(2 * P * a, 2 * P * (a + 1))
-                logp = sb.tile([P, 2 * P], F32, name="logp%d%d" % (h, a))
-                nc.scalar.activation(out=logp[:], in_=totals[h][:, cols], func=ACT.Ln, scale=W_INNER, bias=0.001)
-                nll = sb.tile([P, 2 * P], F32, name="nll%d%d" % (h, a))
+        for a in range(PAIRS):
+            for h in range(HALVES):
+                logp = sb.tile([P, 2 * P], F32, name="logp%d%d" % (a, h))
+                nc.scalar.activation(out=logp[:], in_=totals[a][:, h, :], func=ACT.Ln, scale=W_INNER, bias=0.001)
+                nll = sb.tile([P, 2 * P], F32, name="nll%d%d" % (a, h))
                 nc.vector.tensor_scalar(nll[:], logp[:], -1.0, None, ALU.mult)
-                nc.sync.dma_start(out[h * P : (h + 1) * P, cols], nll[:])
+                nc.sync.dma_start(out[h * P : (h + 1) * P, 2 * P * a : 2 * P * (a + 1)], nll[:])

@@ -72,13 +72,13 @@ def tile_picked_yghqlr_nll_p_kernel(tc, x_words, x_scales, w1, w2, offset, lab, 
         nc.vector.tensor_copy(x_scale[:], scale_table[:].indirect(offsets[:]))
         w2_codes, w2_scales = quantize(w2_grouped, "w2")
 
-        def product(dst, x_codes, t, codes, scales):
+        def product(dst, left, left_scales, right, right_scales):
             nc.tensor.matmul_mx(
                 out=dst,
-                lhsT=x_codes[:].bitcast(FP8X4),
-                lhsT_scale=x_scale[:, t * P : (t + 1) * P],
-                rhs=codes[:].bitcast(FP8X4),
-                rhs_scale=scales[:],
+                lhsT=left.bitcast(FP8X4),
+                lhsT_scale=left_scales,
+                rhs=right.bitcast(FP8X4),
+                rhs_scale=right_scales,
                 start=True,
                 stop=True,
             )
@@ -92,7 +92,9 @@ def tile_picked_yghqlr_nll_p_kernel(tc, x_words, x_scales, w1, w2, offset, lab, 
             x_codes = sb.tile([P, P], U32, name="x_codes%d" % t, align_bytes=64)
             nc.vector.tensor_copy(x_codes[:], word_table[:].bitcast(U32).indirect(offsets[:, 8 * t : 8 * (t + 1)]))
             bank = ps.tile([P, 2, N], F32, name="y%d" % t)
-            product(bank[:, 0, :], x_codes, t, w2_codes, w2_scales)
+            for h in range(HALVES):
+                sites = slice(h * P, (h + 1) * P)
+                product(bank[:, 0, sites], w2_codes[:, sites], w2_scales[:, sites], x_codes[:], x_scale[:, t * P : (t + 1) * P])
             nc.scalar.activation(out=sig_neg[:, t, :], in_=bank[:, 0, :], func=ACT.Sigmoid, scale=-1.0)
             x_tiles.append(x_codes)
             banks.append(bank)
@@ -107,12 +109,17 @@ def tile_picked_yghqlr_nll_p_kernel(tc, x_words, x_scales, w1, w2, offset, lab, 
         nc.vector.tensor_scalar(sign_col[:], cols_bank[:, TILES : 2 * TILES], 2.0, -1.0, ALU.mult, ALU.add)
         w1_codes, w1_scales = quantize(w1_grouped, "w1")
 
-        mean = work("mean")
+        mean_t = work("mean_t")
+        means = [ps.tile([P, 2, N], F32, name="mean%d" % a) for a in range(PAIRS)]
         for t in range(TILES):
-            product(banks[t][:, 1, :], x_tiles[t], t, w1_codes, w1_scales)
+            product(banks[t][:, 1, :], x_tiles[t][:], x_scale[:, t * P : (t + 1) * P], w1_codes[:], w1_scales[:])
+        for t in range(TILES):
             nc.vector.tensor_scalar(
-                mean[:, t, :], banks[t][:, 1, :], off_col[:, t : t + 1], sign_col[:, t : t + 1], ALU.add, ALU.mult
+                mean_t[:, t, :], banks[t][:, 1, :], off_col[:, t : t + 1], sign_col[:, t : t + 1], ALU.add, ALU.mult
             )
+            for h in range(HALVES):
+                sites = slice(h * P, (h + 1) * P)
+                nc.tensor.transpose(means[t // 2][:, t % 2, sites], mean_t[:, t, sites], ident[:])
 
         log_sig = work("log_sig")
         soft = work("soft")
@@ -125,37 +132,28 @@ def tile_picked_yghqlr_nll_p_kernel(tc, x_words, x_scales, w1, w2, offset, lab, 
         pairs = [slice(2 * a, 2 * a + 2) for a in range(PAIRS)]
         args = [work("arg%d" % i) for i in range(4)]
         sigs = [work("sig%d" % i) for i in range(4)]
-        for a in range(PAIRS):
-            for i, c in enumerate(NODES):
-                nc.vector.scalar_tensor_tensor(
-                    out=args[i][:, pairs[a]],
-                    in0=soft[:, pairs[a]],
-                    scalar=0.8 * c,
-                    in1=mean[:, pairs[a]],
-                    op0=ALU.mult,
-                    op1=ALU.add,
-                )
-                nc.scalar.activation(out=sigs[i][:, pairs[a]], in_=args[i][:, pairs[a]], func=ACT.Sigmoid, bias=0.3 * c)
 
-        totals = [ps.tile([P, HALVES, 2 * P], F32, name="total%d" % a) for a in range(PAIRS)]
-
-        def add_turned(part, a, first, last):
-            for h in range(HALVES):
-                for i in range(2):
-                    nc.tensor.matmul(
-                        totals[a][:, h, i * P : (i + 1) * P],
-                        lhsT=part[:, 2 * a + i, h * P : (h + 1) * P],
-                        rhs=ident[:],
-                        is_transpose=True,
-                        start=(first and h == 0 and i == 0),
-                        stop=(last and h == HALVES - 1 and i == 1),
-                    )
+        def node(i, a):
+            nc.vector.scalar_tensor_tensor(
+                out=args[i][:, pairs[a]],
+                in0=soft[:, pairs[a]],
+                scalar=0.8 * NODES[i],
+                in1=means[a][:],
+                op0=ALU.mult,
+                op1=ALU.add,
+            )
+            nc.scalar.activation(out=sigs[i][:, pairs[a]], in_=args[i][:, pairs[a]], func=ACT.Sigmoid, bias=0.3 * NODES[i])
 
         outer = work("outer")
-        three = work("three")
         for a in range(PAIRS):
-            nc.vector.tensor_tensor(outer[:, pairs[a]], sigs[0][:, pairs[a]], sigs[1][:, pairs[a]], ALU.add)
-            add_turned(sigs[3], a, True, False)
+            node(0, a)
+            node(1, a)
+            nc.gpsimd.tensor_tensor(outer[:, pairs[a]], sigs[0][:, pairs[a]], sigs[1][:, pairs[a]], ALU.add)
+        for a in range(PAIRS):
+            node(2, a)
+            node(3, a)
+        three = work("three")
+        total = work("total")
         for a in range(PAIRS):
             nc.vector.scalar_tensor_tensor(
                 out=three[:, pairs[a]],
@@ -165,12 +163,15 @@ def tile_picked_yghqlr_nll_p_kernel(tc, x_words, x_scales, w1, w2, offset, lab, 
                 op0=ALU.mult,
                 op1=ALU.add,
             )
-            add_turned(three, a, False, True)
+        for a in range(PAIRS):
+            nc.vector.tensor_tensor(total[:, pairs[a]], three[:, pairs[a]], sigs[3][:, pairs[a]], ALU.add)
 
         for a in range(PAIRS):
             for h in range(HALVES):
-                logp = sb.tile([P, 2 * P], F32, name="logp%d%d" % (a, h))
-                nc.scalar.activation(out=logp[:], in_=totals[a][:, h, :], func=ACT.Ln, scale=W_INNER, bias=0.001)
+                logp = sb.tile([P, 2, P], F32, name="logp%d%d" % (a, h))
+                nc.scalar.activation(
+                    out=logp[:], in_=total[:, pairs[a], h * P : (h + 1) * P], func=ACT.Ln, scale=W_INNER, bias=0.001
+                )
                 nll = sb.tile([P, 2 * P], F32, name="nll%d%d" % (a, h))
-                nc.vector.tensor_scalar(nll[:], logp[:], -1.0, None, ALU.mult)
+                nc.vector.tensor_scalar(nll[:], logp[:].rearrange("p t j -> p (t j)"), -1.0, None, ALU.mult)
                 nc.sync.dma_start(out[h * P : (h + 1) * P, 2 * P * a : 2 * P * (a + 1)], nll[:])

@@ -33,14 +33,14 @@ def tile_picked_yghqlr_nll_p_kernel(tc, x_words, x_scales, w1, w2, offset, lab, 
         ps = ctx.enter_context(tc.psum_pool(name="ps", bufs=1))
 
         scale_table = sb.tile([P, T], U8, name="scale_table", align_bytes=64)
-        nc.gpsimd.memset(scale_table[:].bitcast(I32), 0)
+        nc.vector.memset(scale_table[:].bitcast(I32), 0)
 
         w2_raw = sb.tile([P, 4, N], F32, name="w2_raw")
         nc.sync.dma_start(w2_raw[:], w2.rearrange("(p j) n -> p j n", j=4))
-        for r in range(4):
-            nc.sync.dma_start(scale_table[r:P:32, :].bitcast(I32), x_scales[0, r:16:4, :].bitcast(I32))
         offsets = sb.tile([P, S // 16], U16, name="offsets")
         nc.sync.dma_start(offsets[:], offs)
+        for r in range(4):
+            nc.sync.dma_start(scale_table[r:P:32, :].bitcast(I32), x_scales[0, r:16:4, :].bitcast(I32))
         word_table = sb.tile([P, T], I32, name="word_table", align_bytes=64)
         nc.sync.dma_start(word_table[:], x_words[0].rearrange("p c r -> p (c r)").bitcast(I32))
         w1_raw = sb.tile([P, 4, N], F32, name="w1_raw")
@@ -69,8 +69,8 @@ def tile_picked_yghqlr_nll_p_kernel(tc, x_words, x_scales, w1, w2, offset, lab, 
 
         w2_grouped = interleave(w2_raw, "w2")
         x_scale = sb.tile([P, S], U8, name="x_scale", align_bytes=64)
-        nc.vector.tensor_copy(x_scale[:], scale_table[:].indirect(offsets[:]))
         w2_codes, w2_scales = quantize(w2_grouped, "w2")
+        nc.vector.tensor_copy(x_scale[:], scale_table[:].indirect(offsets[:]))
 
         def product(dst, left, left_scales, right, right_scales):
             nc.tensor.matmul_mx(

from contextlib import ExitStack

import concourse.mybir as mybir
from concourse.masks import make_identity

K, T, S, N = 512, 2048, 512, 256
FLOPS = 2 * 2 * K * N * S
BYTES = K * T + 16 * T + 2 * K * N * 4 + 2 * S * 4 + 128 * 32 * 2 + N * S * 4

F32 = mybir.dt.float32
BF16 = mybir.dt.bfloat16
I32 = mybir.dt.int32
U32 = mybir.dt.uint32
U16 = mybir.dt.uint16
U8 = mybir.dt.uint8
FP8X4 = mybir.dt.float8_e4m3fn_x4
ALU = mybir.AluOpType
ACT = mybir.ActivationFunctionType

P = 128
TILES = S // P
HALVES = N // P
PAIRS = 2
NODES = (-2.3344, 2.3344, -0.7420, 0.7420)
W_OUTER, W_INNER = 0.0459, 0.4541
TINY = 2.0 ** -60


def tile_picked_yghqlr_nll_p_kernel(tc, x_words, x_scales, w1, w2, offset, lab, offs, out):
    nc = tc.nc
    with ExitStack() as ctx:
        sb = ctx.enter_context(tc.tile_pool(name="sb", bufs=1))
        ps = ctx.enter_context(tc.psum_pool(name="ps", bufs=1))

        scale_table = sb.tile([P, T], U8, name="scale_table", align_bytes=64)
        nc.vector.memset(scale_table[:].bitcast(I32), 0)

        w2_raw = sb.tile([P, 4, N], F32, name="w2_raw")
        nc.sync.dma_start(w2_raw[:], w2.rearrange("(p j) n -> p j n", j=4))
        offsets = sb.tile([P, S // 16], U16, name="offsets")
        nc.sync.dma_start(offsets[:], offs)
        for r in range(4):
            nc.sync.dma_start(scale_table[r:P:32, :].bitcast(I32), x_scales[0, r:16:4, :].bitcast(I32))
        word_table = sb.tile([P, T], I32, name="word_table", align_bytes=64)
        nc.sync.dma_start(word_table[:], x_words[0].rearrange("p c r -> p (c r)").bitcast(I32))
        w1_raw = sb.tile([P, 4, N], F32, name="w1_raw")
        nc.sync.dma_start(w1_raw[:], w1.rearrange("(p j) n -> p j n", j=4))

        ident = sb.tile([P, P], F32, name="ident")
        make_identity(nc, ident[:])
        rows = sb.tile([P, P], F32, name="rows")
        nc.gpsimd.memset(rows[:], 0.0)
        nc.sync.dma_start(rows[0:TILES, :], offset[0].rearrange("(t p) -> t p", p=P))
        nc.sync.dma_start(rows[TILES : 2 * TILES, :], lab[0].rearrange("(t p) -> t p", p=P))

        def interleave(raw, name):
            grouped = sb.tile([P, N, 4], BF16, name=name + "_grouped", align_bytes=64)
            nc.vector.tensor_copy(
                out=grouped[:].rearrange("p (c i) j -> p c j i", i=4),
                in_=raw[:].rearrange("p j (c i) -> p c j i", i=4),
            )
            return grouped

        def quantize(grouped, name):
            codes = sb.tile([P, N], U32, name=name + "_codes", align_bytes=64)
            scales = sb.tile([P, N], U8, name=name + "_scales", align_bytes=64)
            nc.vector.quantize_mx(out=codes[:].bitcast(FP8X4), scales=scales[:], in_=grouped[:].rearrange("p n j -> p (n j)"))
            return codes, scales

        w2_grouped = interleave(w2_raw, "w2")
        x_scale = sb.tile([P, S], U8, name="x_scale", align_bytes=64)
        w2_codes, w2_scales = quantize(w2_grouped, "w2")
        nc.vector.tensor_copy(x_scale[:], scale_table[:].indirect(offsets[:]))

        def product(dst, left, left_scales, right, right_scales):
            nc.tensor.matmul_mx(
                out=dst,
                lhsT=left.bitcast(FP8X4),
                lhsT_scale=left_scales,
                rhs=right.bitcast(FP8X4),
                rhs_scale=right_scales,
                start=True,
                stop=True,
            )

        def work(name):
            return sb.tile([P, TILES, N], F32, name=name)

        sig_neg = work("sig_neg")
        x_tiles, banks = [], []
        for t in range(TILES):
            x_codes = sb.tile([P, P], U32, name="x_codes%d" % t, align_bytes=64)
            nc.vector.tensor_copy(x_codes[:], word_table[:].bitcast(U32).indirect(offsets[:, 8 * t : 8 * (t + 1)]))
            bank = ps.tile([P, 2, N], F32, name="y%d" % t)
            for h in range(HALVES):
                sites = slice(h * P, (h + 1) * P)
                product(bank[:, 0, sites], w2_codes[:, sites], w2_scales[:, sites], x_codes[:], x_scale[:, t * P : (t + 1) * P])
            nc.scalar.activation(out=sig_neg[:, t, :], in_=bank[:, 0, :], func=ACT.Sigmoid, scale=-1.0)
            x_tiles.append(x_codes)
            banks.append(bank)

        cols_bank = ps.tile([P, P], F32, name="cols_bank")
        nc.tensor.transpose(cols_bank[:], rows[:], ident[:])
        off_col = sb.tile([P, TILES], F32, name="off_col")
        sign_col = sb.tile([P, TILES], F32, name="sign_col")

        w1_grouped = interleave(w1_raw, "w1")
        nc.vector.tensor_copy(off_col[:], cols_bank[:, 0:TILES])
        nc.vector.tensor_scalar(sign_col[:], cols_bank[:, TILES : 2 * TILES], 2.0, -1.0, ALU.mult, ALU.add)
        w1_codes, w1_scales = quantize(w1_grouped, "w1")

        mean_t = work("mean_t")
        means = [ps.tile([P, 2, N], F32, name="mean%d" % a) for a in range(PAIRS)]
        for t in range(TILES):
            product(banks[t][:, 1, :], x_tiles[t][:], x_scale[:, t * P : (t + 1) * P], w1_codes[:], w1_scales[:])
        for t in range(TILES):
            nc.vector.tensor_scalar(
                mean_t[:, t, :], banks[t][:, 1, :], off_col[:, t : t + 1], sign_col[:, t : t + 1], ALU.add, ALU.mult
            )
            for h in range(HALVES):
                sites = slice(h * P, (h + 1) * P)
                nc.tensor.transpose(means[t // 2][:, t % 2, sites], mean_t[:, t, sites], ident[:])

        log_sig = work("log_sig")
        soft = work("soft")
        for t in range(TILES):
            nc.scalar.activation(out=log_sig[:, t, :], in_=sig_neg[:, t, :], func=ACT.Ln, bias=TINY)
            nc.vector.scalar_tensor_tensor(
                out=soft[:, t, :], in0=log_sig[:, t, :], scalar=-1.0, in1=banks[t][:, 0, :], op0=ALU.mult, op1=ALU.max
            )

        pairs = [slice(2 * a, 2 * a + 2) for a in range(PAIRS)]
        args = [work("arg%d" % i) for i in range(4)]
        sigs = [work("sig%d" % i) for i in range(4)]

        def node(i, a):
            nc.vector.scalar_tensor_tensor(
                out=args[i][:, pairs[a]],
                in0=soft[:, pairs[a]],
                scalar=0.8 * NODES[i],
                in1=means[a][:],
                op0=ALU.mult,
                op1=ALU.add,
            )
            nc.scalar.activation(out=sigs[i][:, pairs[a]], in_=args[i][:, pairs[a]], func=ACT.Sigmoid, bias=0.3 * NODES[i])

        outer = work("outer")
        for a in range(PAIRS):
            node(0, a)
            node(1, a)
            nc.gpsimd.tensor_tensor(outer[:, pairs[a]], sigs[0][:, pairs[a]], sigs[1][:, pairs[a]], ALU.add)
        for a in range(PAIRS):
            node(2, a)
            node(3, a)
        three = work("three")
        total = work("total")
        for a in range(PAIRS):
            nc.vector.scalar_tensor_tensor(
                out=three[:, pairs[a]],
                in0=outer[:, pairs[a]],
                scalar=W_OUTER / W_INNER,
                in1=sigs[2][:, pairs[a]],
                op0=ALU.mult,
                op1=ALU.add,
            )
        for a in range(PAIRS):
            nc.vector.tensor_tensor(total[:, pairs[a]], three[:, pairs[a]], sigs[3][:, pairs[a]], ALU.add)

        for a in range(PAIRS):
            for h in range(HALVES):
                logp = sb.tile([P, 2, P], F32, name="logp%d%d" % (a, h))
                nc.scalar.activation(
                    out=logp[:], in_=total[:, pairs[a], h * P : (h + 1) * P], func=ACT.Ln, scale=W_INNER, bias=0.001
                )
                nll = sb.tile([P, 2 * P], F32, name="nll%d%d" % (a, h))
                nc.vector.tensor_scalar(nll[:], logp[:].rearrange("p t j -> p (t j)"), -1.0, None, ALU.mult)
                nc.sync.dma_start(out[h * P : (h + 1) * P, 2 * P * a : 2 * P * (a + 1)], nll[:])
